import numpy as np, ml_dtypes
CORES = [1,5,17,21,33,37,49,53]
N = 8
BF = ml_dtypes.bfloat16
def gentries(a):
    return np.ascontiguousarray(a.reshape(8, 16, -1).transpose(0, 2, 1)).reshape(8, -1)
def gtable(e):
    e = np.asarray(e); return np.ascontiguousarray(e.reshape(8, -1, 16).transpose(0, 2, 1)).reshape(128, -1).astype(np.int32)
P, BS, T, CAP, G = 4352, 768, 3, 256, 96
S, SB, NEED, KILL = 4, 2, 10, 1
W = P + (N - 1) * G
def clans(rng, kk):
    sc = rng.choice(np.array([191.0, 120.0, 60.0], np.float32), (8, 1, 1)); cen = (sc * rng.random((8, 16, 4))).astype(np.float32); cen[:, :, 0] *= np.float32(0.1)
    t = np.maximum(1, (sc * (0.06 + 0.08 * rng.random((N, 8, 16, 1)))).astype(np.int32)); off = rng.integers(0, 4, (8, 1))
    def near():
        who = ((rng.random((N, 8, P)) * kk[:, None]).astype(np.int64) + off) & 3
        w = sc * (np.float32(0.05) + np.float32(0.15) * rng.random((N, 8, 1, P), dtype=np.float32))
        v = np.take_along_axis(np.broadcast_to(cen, (N, 8, 16, 4)), who[:, :, None, :], 3) + w * (2 * rng.random((N, 8, 16, P), dtype=np.float32) - 1)
        return np.clip(np.rint(v), 0, 191).astype(np.int32)
    x = near(); share = KILL * kk[:, None, None] * rng.choice(np.array([0.03, 0.06, 0.09]), (N, 8, 1, 1))
    y = np.where(rng.random((N, 8, 1, P)) < 0.1, 255, rng.integers(0, 192, (N, 8, 16, P), dtype=np.int32))
    return x, np.where(rng.random((N, 8, 1, P)) < share, near(), y), t
def chosen(key):
    return np.ascontiguousarray(np.argsort(key, axis=-1)[..., :16 * BS])
def deal(pts, num):
    a = np.empty((16, BS), np.int64); a[:, pts] = num.reshape(BS, 16).T
    return a.reshape(-1)
def parts(rng):
    x, y, t = clans(rng, rng.permutation(np.array([1, 1, 2, 2, 2, 3, 3, 4])))
    sd = rng.random((N, 8, BS)) < rng.choice(np.array([0.2, 0.4, 0.6, 0.9]), (N, 8, 1))
    c = chosen(rng.random((N, 8, T, S * W), dtype=np.float32))
    b = np.argsort(rng.random((N, 8, P)) * np.where(np.arange(P) < T * BS, 0.6, 1.0), axis=-1)[..., :(N - 1) * G]
    return x, y, t, sd, c, np.ascontiguousarray(b)
def pack(x, y, t, sd, c, b):
    c = c.reshape(N, 8, T, 16, BS).transpose(0, 1, 3, 2, 4).reshape(N, 128, T * BS)
    return {"x": x.reshape(N, 128, P).astype(np.float32).astype(BF), "y0": y.reshape(N, 128, P).astype(np.float32).astype(BF),
            "tl": t.reshape(N, 128, 1).astype(np.float32).astype(BF), "sd": sd.astype(np.float32).astype(BF),
            "cd": np.ascontiguousarray(c).astype(np.int32), "snd": np.stack([gtable(a) for a in b])}
def setup_inputs(rng):
    return pack(*parts(rng))
def setup_inputs_room(rng):
    x, y, t, sd, c, b = parts(rng)
    o = np.argsort(np.argsort(rng.random((N, 8, BS)), axis=-1), axis=-1); n = rng.choice(np.array([0, 1, CAP - 1, CAP, CAP + 1, BS]), (N, 8))
    n[0] = (CAP, CAP + 1, BS, CAP - 1, 1, 0, CAP, BS); n[1] = (BS, CAP, CAP + 1, CAP, CAP - 1, CAP, 0, 1)
    return pack(x, y, t, o < n[..., None], c, b)
def setup_inputs_ties(rng):
    x, y, t, sd, c, b = parts(rng)
    t = np.tile(rng.integers(0, 21, (1, 8, 16, 1)), (N, 1, 1, 1)); base = rng.integers(10, 121, (8, 16, 1))
    def step():
        return base + t * rng.integers(0, 3, (N, 8, 16, P), dtype=np.int32) + (rng.random((N, 8, 16, P), dtype=np.float32) < 0.3)
    x = step(); y = np.where(rng.random((N, 8, 1, P)) < 0.1 * KILL, step(), 255)
    t[:, 0] = 63; x[:, 0] = rng.choice(np.array([127, 128, 191]), (N, 16, P)); y[:, 0] = rng.choice(np.array([255, 255, 255, 191, 128, 64]), (N, 16, P))
    return pack(x, y, t, sd, c, b)
def setup_inputs_ends(rng):
    x, y, t, sd, c, b = parts(rng); a = np.arange(S * W); n = np.arange(BS); k = np.arange((N - 1) * G)
    key = rng.random((N, 8, T, S * W), dtype=np.float32)
    key[:, 1::2, :, S * P:] -= 1; key[:, 1::2, :, :S] -= 1; key[:, 1::2, :, S * (P - 1):S * P] -= 1
    key[:, 2] += (a >= 16 * BS).astype(np.float32); key[:, 4] += (a < S * W - 16 * BS).astype(np.float32)
    c = rng.permuted(chosen(key), axis=-1); c[:, 6] = np.arange(16 * BS)
    b[:, 1] = k; b[:, 3] = P - 1 - k; b[:, 7] = T * BS - (N - 1) * G + k
    sd[:, ::2] = n >= BS - CAP; sd[:, 1::2] = (n & 1) == 0; sd[:, 5] = (n == 0) | (n == BS - 1)
    return pack(x, y, t, sd, c, b)
def setup_inputs_dark(rng):
    x, y, t, sd, c, b = parts(rng); q = rng.permutation(N); g = rng.permutation(8)
    y[:, g[1]] = 255; t[:, g[2]] = 0
    for j in g[3:7]:
        x[:, j] = x[:, j] & 31; t[:, j] = 63
    y[:, g[3]] = y[:, g[3]] & 31; y[:, g[4]] = 128 + (y[:, g[4]] & 63)
    for r in range(N):
        m = np.isin(np.arange(BS) & 15, rng.permutation(16)[:16 * CAP // BS]); sd[r, g[4]] = m
        num = np.concatenate([rng.permutation(np.arange(S * P, S * W)), np.arange(16 * BS - S * (W - P))])
        c[r, g[4], 0] = deal(np.argsort(rng.random(BS) - m), num)
        m = rng.permutation(BS) < CAP; sd[r, g[5]] = m; o = rng.permutation(16)
        pl = np.argsort(o[np.arange(W) & 15] + rng.random(W))[:16 * CAP]; num = rng.permutation(S * pl + rng.integers(0, S, 16 * CAP))
        num = np.concatenate([num, rng.permutation(np.setdiff1d(np.arange(S * W), num))])[:16 * BS]
        c[r, g[5], 0] = deal(np.argsort(rng.random(BS) - m), num)
    c[:, g[4], 1:] = rng.permuted(np.tile(np.arange(16 * BS), (N, T - 1, 1)), axis=-1)
    key = rng.random((N, S * W)); key[:, S * BS:2 * S * BS] += 1; c[:, g[6], 0] = chosen(key)
    b[:, g[6]] = np.argsort(rng.random((N, P)) + (np.arange(P) // BS == 1), axis=-1)[:, :(N - 1) * G]
    sd[:, g[0]] = False; sd[q[0]] = False; sd[q[1], g[3]] = True
    return pack(x, y, t, sd, c, b)
def setup_inputs_spread(rng):
    x, y, t, sd, c, b = parts(rng)
    x = np.minimum((np.exp2(7.59 * rng.random((N, 8, 1, P))) * rng.random((N, 8, 16, P))).astype(np.int32), 191)
    y = np.minimum((np.exp2(7.59 * rng.random((N, 8, 1, P))) * rng.random((N, 8, 16, P))).astype(np.int32), 191)
    y = np.where(rng.random((N, 8, 1, P)) < rng.choice(np.array([0.1, 0.5, 0.9]), (N, 8, 1, 1)), 255, y)
    low = np.arange(16)[:, None] == rng.integers(0, 16, (N, 8, 1, P))
    y = np.where(rng.random((N, 8, 1, P)) < 0.15, np.where(low, y >> 3, 255), y)
    t = np.rint(np.exp2(6 * rng.random((N, 8, 16, 1)))).astype(np.int32) - 1
    return pack(x, y, np.minimum(t, 63), rng.random((N, 8, BS)) < rng.random((N, 8, 1)), c, b)
def check_inputs(d):
    bad = []
    for k, hi in (("x", 191), ("y0", 191), ("tl", 63), ("sd", 1)):
        v = np.asarray(d[k]).astype(np.float32); ok = (v >= 0) & (v <= hi) & (v == np.floor(v))
        if k == "y0": ok = ok | (v == 255)
        if not np.all(ok): bad.append("range of " + k)
    for k, hi in (("cd", S * W - 1), ("snd", P - 1)):
        if np.min(d[k]) < 0 or np.max(d[k]) > hi: bad.append("range of " + k)
    c = np.sort(np.asarray(d["cd"]).reshape(N, 8, 16, T, BS).transpose(0, 1, 3, 2, 4).reshape(N, 8, T, 16 * BS), axis=-1)
    if np.any(c[..., 1:] == c[..., :-1]): bad.append("equal numbers in a brood of cd")
    s = np.sort(np.stack([gentries(a) for a in d["snd"]]), axis=-1)
    if np.any(s[..., 1:] == s[..., :-1]): bad.append("equal numbers in snd")
    return bad
def windows(a, sl):
    res = []
    for r in range(N):
        w = [a[r]]
        for d in range(1, N):
            q = (r - d) % N; w.append(np.take_along_axis(a[q], sl[q, :, d - 1][:, None, :], 2))
        res.append(np.concatenate(w, axis=2))
    return np.stack(res)
def matches(come, xn, t):
    return np.add.reduce((np.abs(come - xn[:, None, :]) <= t[:, :, None]).astype(np.int64), axis=0) >= NEED
def reference(x, y0, tl, sd, cd, snd):
    X = x.astype(np.float32).astype(np.int32).reshape(N, 8, 16, P); Y = y0.astype(np.float32).astype(np.int32).reshape(N, 8, 16, P)
    t = tl.astype(np.float32).astype(np.int32).reshape(N, 8, 16, 1)
    C = (cd.astype(np.int64) >> SB).reshape(N, 8, 16, T * BS); sl = np.stack([gentries(a) for a in snd]).astype(np.int64).reshape(N, 8, N - 1, G)
    flag = np.zeros((N, 8, P), bool); flag[:, :, :BS] = sd.astype(np.float32) > 0.5; member = np.zeros((N, 8, P), bool)
    xw = windows(X, sl)
    for s in range(T):
        fl = flag[:, :, s * BS:(s + 1) * BS]
        member[:, :, s * BS:(s + 1) * BS] = fl & (np.add.accumulate(fl.astype(np.int64), axis=2) <= CAP)
        new = np.zeros((N, 8, W), bool)
        for r in range(N):
            for g in range(8):
                n = np.flatnonzero(member[r, g, s * BS:(s + 1) * BS]) + s * BS; c = C[r, g][:, n]
                come = xw[r, g][:, c.reshape(-1)].reshape(16, 16, len(n))
                new[r, g][c[matches(come, X[r, g][:, n], t[r, g])]] = True
        for r in range(N):
            flag[r] |= new[r, :, :P]
            for d in range(1, N):
                q = (r - d) % N
                for g in range(8): flag[q, g, sl[q, g, d - 1][new[r, g, P + (d - 1) * G:P + d * G]]] = True
    for s in range(T - 1, -1, -1):
        yw = windows(Y, sl); Z = Y.copy()
        for r in range(N):
            for g in range(8):
                n = np.flatnonzero(member[r, g, s * BS:(s + 1) * BS]) + s * BS; c = C[r, g][:, n]; xn = X[r, g][:, n]
                come = yw[r, g][:, c.reshape(-1)].reshape(16, 16, len(n))
                dead = np.add.reduce(matches(come, xn, t[r, g]).astype(np.int64), axis=0) >= KILL
                Z[r, g][:, n] = np.where(dead, 255, (xn + np.minimum(191, np.minimum.reduce(come, axis=1))) >> 1)
        Y = Z
    return {"yv": np.ascontiguousarray(Y[:, :, :, :T * BS]).reshape(N, 128, T * BS).astype(np.float32).astype(BF), "yf": np.where(member, 2, flag.astype(np.int64)).astype(np.float32).astype(BF)}

from concourse.bass import DstId, RemoteDMATransfer
from concourse.mybir import AluOpType, ActivationFunctionType

P, BS, GB, NR = 4352, 768, 96, 8
NB = 7 * GB
W = P + NB
WX = W + 128
VW = 4 * W + 512
C = 512
NC = 8


def _sb(n, d):
    return ("sbuf", [128, n], d)


_BF = {"xw": WX, "yA": WX, "yB": WX, "wA": VW, "wB": VW, "E": 2048, "L": 2048, "I": 128, "BO": 128, "NU": 128, "ga": 4096, "mn": 4096,
       "sm": C, "sx": C, "row": P, "tlb": 1, "g2": 1024, "cwin": 1024, "sf0": NB, "sf1": NB, "sb": NB, "gb": BS, "rbq": 272, "sdq": 272,
       "mq": 272, "yfo": 272, "yft": 272, "F2a": 48, "z48": 48, "F": 48, "cs": 48, "dd": 128}
_F32 = {"L32": 2048, "inv": P, "NF": 48, "A": 48, "q1": 48, "q2": 48, "q3": 48, "N769": 48, "N257": 48, "N256": 48, "pf15": 8, "pf15k": 8}
_I32 = {"pk": 3 * BS, "pkw": 1544, "dum": 256, "ta": 256, "tb": 256, "sndi": 42, "pi": 8, "pj": 8, "s32": 128, "h32": 128}
_U16 = {"invT": 96, "sndu": 48, "P16": 48}
for _s in range(3):
    _BF.update({"zc%d" % _s: 1024, "xm%d" % _s: 256, "nx%d" % _s: 256, "tq%d" % _s: 1088, "fr%d" % _s: 688, "ab%d" % _s: C, "id%d" % _s: C, "mt%d" % _s: C})
    _F32.update({"P32_%d" % _s: 48})
    _U16.update({"vu%d" % _s: 256, "cu%d" % _s: 256, "yp%d" % _s: 48})
SCRATCH = {}
for _t, _d in ((_BF, "bfloat16"), (_F32, "float32"), (_I32, "int32"), (_U16, "uint16")):
    SCRATCH.update({_n: _sb(_c, _d) for _n, _c in _t.items()})
PSUMS = ["ps0", "ps1", "ps2", "pc0", "pc1", "pr0", "pr1", "pf"]
for _n in PSUMS:
    SCRATCH[_n] = ("psum", [128, 512], "float32")
NDMA = 30
EXCH = ["x", "f0", "f1", "f2", "y0", "y1", "y2"]
SEMAPHORES = ["sv", "sa", "st", "sg"] + ["d%d" % k for k in range(NDMA)] + ["r_" + e for e in EXCH] + ["l_" + e for e in EXCH]
EG_OUT = "ssvsssss"
EG_OUT2 = "ssssssss"
EG_BACK2 = "sssssvss"
EG_BACK = "vsssssss"
SPLIT = 4
ZB, ZV, ZS = 8000, 9000, 6000


def exchange_plan(topo, cores, r, sg):
    src = cores[r]
    dst = [None] + [cores[(r + sg * d) % NR] for d in range(1, NR)]
    off = [d for d in range(1, NR) if topo.chip(dst[d]) != topo.chip(src)]
    on = [d for d in range(1, NR) if d not in off]
    eng = topo.engines(src, dst[off[0]])
    n = len(eng)
    first, second = off[:4], off[4:]
    calls = [[(d, eng[i * n // 4:(i + 1) * n // 4]) for i, d in enumerate(first)],
             [(d, eng[i * n // 2:(i + 1) * n // 2]) for i, d in enumerate(second)]]
    for d in on:
        free = [e for e in topo.engines(src, dst[d]) if e not in eng]
        calls[0 if d < second[0] else 1].append((d, free[:8]))
    return calls


def rank_program(g, core, T, topo):
    rank = T.rank_of(core)
    if rank is None:
        return
    OP, AF = AluOpType, ActivationFunctionType
    cores = list(T.cores)
    eng = {"g": g, "vector": g.vector, "scalar": g.scalar, "tensor": g.tensor, "sync": g.sync}
    csem = {"vector": "sv", "scalar": "sa", "tensor": "st", "g": "sg"}
    count, totals, recs, ndma, seq = {}, {}, {}, [0], [0]
    known = {q: {} for q in eng}

    def B(name, lo=None, hi=None, st=1, parts=None):
        lo = 0 if lo is None else lo
        hi = SCRATCH[name][1][1] if hi is None else hi
        ap = T[name][:, lo:hi:st] if parts is None else T[name][parts, lo:hi:st]
        return {"ap": ap, "r": [(name, lo, hi)], "x": []}

    def IND(win, off):
        return {"ap": win["ap"].indirect(off["ap"]), "r": win["r"], "x": off["r"]}

    def HB(ap):
        return {"ap": ap, "r": [], "x": []}

    def need_of(q, reads, writes):
        need = []
        for acc, w in [(a, False) for a in reads] + [(a, True) for a in writes]:
            name, lo, hi = acc
            psum = name in PSUMS
            for rec in recs.get(name, []):
                if (rec["hi"] <= lo or rec["lo"] >= hi) and not psum:
                    continue
                if rec["q"] == q and q == "tensor":
                    continue
                if w or rec["w"] or (psum and rec["q"] != q):
                    need.append(rec["tok"])
        return need

    def do_waits(q, need):
        K = known[q]
        best = {}
        for tok in need:
            s = tok["sem"]
            if K.get(s, 0) < tok["val"] and (s not in best or best[s]["val"] < tok["val"]):
                best[s] = tok
        for s in sorted(best):
            if any(o != s and best[o]["clk"].get(s, 0) >= best[s]["val"] for o in best):
                del best[s]
        for s in sorted(best):
            eng[q].wait_ge(T.sem[s], best[s]["val"])
            for a, b in best[s]["clk"].items():
                K[a] = max(K.get(a, 0), b)

    def record(q, tok, reads, writes):
        for name, lo, hi in writes:
            keep = [x for x in recs.get(name, []) if not (name in PSUMS or (x["lo"] >= lo and x["hi"] <= hi))]
            recs[name] = keep + [{"lo": lo, "hi": hi, "w": True, "tok": tok, "q": q}]
        for name, lo, hi in reads:
            recs.setdefault(name, []).append({"lo": lo, "hi": hi, "w": False, "tok": tok, "q": q})

    def op(q, fn, outs, ins):
        reads = [a for o in ins for a in o["r"] + o["x"]] + [a for o in outs for a in o["x"]]
        writes = [a for o in outs for a in o["r"]]
        do_waits(q, need_of(q, reads, writes))
        s = csem[q]
        count[s] = count.get(s, 0) + 1
        fn(eng[q]).then_inc(T.sem[s], 1)
        clk = dict(known[q])
        clk[s] = count[s]
        record(q, {"sem": s, "val": count[s], "clk": clk}, reads, writes)

    def dma(q, out, in_, after=()):
        do_waits(q, need_of("dma", in_["r"], out["r"]) + list(after))
        s = "d%d" % ndma[0]
        ndma[0] += 1
        eng[q].dma_start(out["ap"], in_["ap"]).then_inc(T.sem[s], 16)
        clk = dict(known[q])
        clk[s] = totals[s] = 16
        record("dma", {"sem": s, "val": 16, "clk": clk}, in_["r"], out["r"])

    def send(name, src, land, at, sg=1):
        ls, rs = "l_" + name, "r_" + name
        done, pend, clk = 0, [], {}
        for call in exchange_plan(topo, cores, rank, sg):
            tr, reads = [], []
            for d, es in call:
                to = cores[(rank + sg * d) % NR]
                rid, pid = topo.addr(to)[:2]
                lo = (d - 1) * GB
                reads.append((src, lo, lo + GB))
                tr.append(RemoteDMATransfer(dst_ids=[DstId(rid=rid, pnc=pid)], dma_engine_mask=sum(1 << e for e in es), remote_sem=T.sem[rs],
                                            src=T[src][:, lo:lo + GB], dst=T[land][:, at + lo:at + lo + GB]))
                done += len(es)
            do_waits("g", need_of("g", reads, []))
            g.remote_dma_fused(tr, local_sem=T.sem[ls])
            pend += reads
            clk = dict(known["g"])
        clk[ls] = totals[ls] = done
        record("g", {"sem": ls, "val": done, "clk": clk}, pend, [])
        n = sum(len(es) for q in range(NR) if q != rank for call in exchange_plan(topo, cores, q, sg) for d, es in call if (q + sg * d) % NR == rank)
        totals[rs] = n
        rt = {"sem": rs, "val": n, "clk": {rs: n}}
        recs[land] = [x for x in recs.get(land, []) if not (x["lo"] >= at and x["hi"] <= at + NB)] + [{"lo": at, "hi": at + NB, "w": True, "tok": rt, "q": "ext"}]
        return rt

    def copy(out, in_): op("vector", lambda e: e.tensor_copy(out["ap"], in_["ap"]), [out], [in_])
    def tt(out, a, b, o): op("vector", lambda e: e.tensor_tensor(out["ap"], a["ap"], b["ap"], o), [out], [a, b])
    def fill(out, v): op("vector", lambda e: e.memset(out["ap"], v), [out], [])

    def ts(out, a, s1, o1, s2=None, o2=None):
        col = isinstance(s1, dict)
        v1 = s1["ap"] if col else s1
        ins = [a, s1] if col else [a]
        if o2 is None:
            op("vector", lambda e: e.tensor_scalar(out["ap"], a["ap"], v1, None, o1), [out], ins)
        else:
            op("vector", lambda e: e.tensor_scalar(out["ap"], a["ap"], v1, s2, o1, o2), [out], ins)

    def scan(out, d0, d1, o0, o1):
        op("vector", lambda e: e.tensor_tensor_scan(out["ap"], d0["ap"], d1["ap"], 0.0, o0, o1), [out], [d0, d1])

    def act(out, in_, f, **kw): op("scalar", lambda e: e.activation(out["ap"], in_["ap"], f, **kw), [out], [in_])

    def take(q, out, win, off):
        if q == "v":
            copy(out, IND(win, off))
        else:
            act(out, IND(win, off), AF.Copy)

    def pe(mms):
        def run_all(e):
            for o, l, r, a, b in mms:
                k = e.matmul(o["ap"], l["ap"], r["ap"], a, b)
            return k
        outs, ins = {}, {}
        for o, l, r, a, b in mms:
            outs[o["r"][0]] = o
            ins[l["r"][0]] = l
            ins[r["r"][0]] = r
        op("tensor", run_all, list(outs.values()), list(ins.values()))

    def chain(out, pairs, first=True, last=True):
        n = len(pairs)
        return [(out, l, r, first and i == 0, last and i == n - 1) for i, (l, r) in enumerate(pairs)]

    def Lm(a, nm="L"):
        return B(nm, 128 * a, 128 * a + 128)

    def gsel(o, pat, cmp, base, cm, i=None):
        i = o if i is None else i
        op("g", lambda e: e.affine_select(o["ap"], i["ap"], pat, cmp, 0.0, base, cm), [o], [i])

    def giota(o, pat, base, cm):
        op("g", lambda e: e.iota(o["ap"], pat, base, cm, allow_small_or_imprecise_dtypes=True), [o], [])

    def zero(win, lo, nv, ns, ng):
        for q, n in (("v", nv), ("s", ns), ("g", ng)):
            end = lo + n
            while lo < end:
                m = end - lo if q == "v" else min(2048, end - lo)
                o = B(win, lo, lo + m)
                if q == "v":
                    fill(o, 0.0)
                elif q == "s":
                    act(o, B("E", 0, m), AF.Copy, scale=0.0)
                else:
                    giota(o, [[0, m]], 0, 0)
                lo += m

    def pack(s):
        o = B("pk", s * BS, s * BS + BS)
        ts(o, o, 256.0, OP.mult)
        tt(o, o, B("xw", s * BS, s * BS + BS), OP.add)

    def members(s):
        pf = B("pf", 0, 48)
        ts(B("F"), pf, 0.5, OP.is_gt)
        scan(B("cs"), B("z48"), B("F"), OP.add, OP.add)
        ts(B("NF"), pf, 0.5, OP.is_le)
        pe(chain(B("pc0", 0, 48), [(B("BO"), B("cs")), (B("NU"), B("F"))]))
        tt(B("A"), B("NF"), B("N769"), OP.mult)
        tt(B("P32_%d" % s), B("pc0", 0, 48), B("A"), OP.max)
        copy(B("P16"), B("P32_%d" % s))
        copy(IND(B("pkw"), B("P16")), B("pk", s * BS, s * BS + BS))
        half_list(s, 0)
        ts(B("tb"), B("pkw", 1, 257), 255, OP.bitwise_and)
        copy(B("xm%d" % s), B("tb"))
        pe([(B("pr0", 128 * h, 128 * h + 128), B("xm%d" % s, 128 * h, 128 * h + 128), B("I"), True, True) for h in range(2)])

    def half_list(s, lo):
        ts(B("ta", lo, lo + 128), B("pkw", 1 + lo, 129 + lo), 10, OP.arith_shift_right)
        copy(B("cu%d" % s, lo, lo + 128), B("ta", lo, lo + 128))

    def members2(s):
        ts(B("nx%d" % s), B("pr0", 0, 256), -1.0, OP.mult)
        half_list(s, 128)

    def numbers(s):
        ts(B("ta"), B("pkw", 1, 257), 8, OP.arith_shift_right)
        copy(B("vu%d" % s), B("ta"))
        if s < 2:
            copy(B("pkw", 1, 257), B("dum"))

    def places(s):
        p = B("P32_%d" % s)
        ts(B("q1"), p, 256.5, OP.is_lt)
        tt(B("q2"), p, B("N257"), OP.subtract)
        tt(B("q3"), B("q2"), B("q1"), OP.mult)
        tt(B("q2"), B("q3"), B("N256"), OP.add)
        copy(B("yp%d" % s), B("q2"))

    def chunks(kind, s, win, ks, eg):
        res = []
        for k in ks:
            i = seq[0]
            seq[0] += 1
            ga = B("g2", C * (i % 2), C * (i % 2) + C) if kind == "o" and s == 2 else B("ga", C * k, C * k + C)
            res.append({"kind": kind, "s": s, "k": k, "i": i, "win": win, "q": eg[k], "ga": ga})
        return res

    def gat(c):
        take(c["q"], c["ga"], B("xw" if c["kind"] == "o" else c["win"]), B("cu%d" % c["s"], 32 * c["k"], 32 * c["k"] + 32))

    def dif(c):
        h, e = 128 * (c["k"] // 4), C * (c["k"] % 4)
        pe(chain(B("ps%d" % (c["i"] % 3)), [(B("nx%d" % c["s"], h, h + 128), B("E", e, e + C)), (B("I"), c["ga"])]))

    def near(c):
        r = c["i"] % 3
        act(B("ab%d" % r), B("ps%d" % r), AF.Abs)
        ts(B("id%d" % r), B("ab%d" % r), B("tlb"), OP.is_le)
        pe(chain(B("pc%d" % (c["i"] % 2)), [(B("BO"), B("id%d" % r))]))
        if c["kind"] == "b":
            scan(B("mn", C * c["k"], C * c["k"] + C), B("sm"), c["ga"], OP.max, OP.min)

    def fin(c):
        s, k, pc = c["s"], c["k"], B("pc%d" % (c["i"] % 2))
        if c["kind"] == "o":
            mt = B("mt%d" % (c["i"] % 3))
            act(mt, pc, AF.Relu, bias=-9.0)
            copy(IND(B(c["win"]), B("vu%d" % s, 32 * k, 32 * k + 32)), mt)
            return
        scan(c["ga"], B("sx"), pc, OP.min, OP.max)
        if k % 4 == 3:
            m, c0 = 128 * (k // 4), 2048 * (k // 4)
            tt(B("s32"), B("mn", c0 + 15, c0 + 2048, 16), B("xm%d" % s, m, m + 128), OP.add)
            ts(B("dd"), B("ga", c0 + 15, c0 + 2048, 16), 9.5, OP.is_ge, 255.0, OP.mult)
            ts(B("h32"), B("s32"), 1, OP.arith_shift_right)
            tt(B("zc%d" % s, m, m + 128), B("h32"), B("dd"), OP.max)

    def run(cs, at={}, after=None):
        n = len(cs)
        for t in range(-2, n + 1):
            early = after and t == NC
            if early:
                fin(cs[t - 1])
                after()
            if t < 0 and t in at:
                at[t]()
            if 0 <= t + 1 < n:
                dif(cs[t + 1])
            if 0 <= t < n:
                near(cs[t])
            if t >= 1 and not early:
                fin(cs[t - 1])
            if t + 2 < n:
                gat(cs[t + 2])
            if t >= 0 and t in at:
                at[t]()

    def border_flags(s, win):
        now, old = "sf%d" % (s % 2), "sf%d" % ((s + 1) % 2)
        cut = (0, 288, 480) if s < 2 else (0, 336, NB)
        for h in range(2):
            a, b = cut[h], cut[h + 1]
            prs = [] if s == 0 else [(B("I"), B(old, a, b))]
            prs += [(B("I"), B(win, 4 * P + 4 * a + k, 4 * P + 4 * b, 4)) for k in range(4)]
            pe(chain(B("pr%d" % h, 0, b - a), prs))
            act(B(now, a, b), B("pr%d" % h, 0, b - a), AF.Copy)
        if s < 2:
            st = [B(win, 4 * P + 4 * 480 + k, 4 * W, 4) for k in range(4)]
            m0, m1, o = B("mt0", 0, 192), B("mt1", 0, 192), B(now, 480, NB)
            tt(m0, st[0], st[1], OP.add)
            tt(m1, st[2], st[3], OP.add)
            if s:
                tt(m0, m0, B(old, 480, NB), OP.add)
            tt(o, m0, m1, OP.add)
        send("f%d" % s, now, "fr%d" % s, 0, -1)

    def brood_table(t, win):
        o = 4 * BS * t
        return [(Lm(a), B(win, o + 4 * a + k, o + 4 * BS, 64)) for a in range(16) for k in range(4)]

    def flags_in(s):
        win = B("fr%d" % s)
        o = 48 * s
        take("s", B("gb", 0, 384), win, B("invT", o, o + 24))
        take("v", B("gb", 384, BS), win, B("invT", o + 24, o + 48))
        pe(chain(B("pf", 0, 48), [(Lm(a), B("gb", a, BS, 16)) for a in range(16)], first=False))

    def stand(s, nxt):
        take("s", B(nxt, BS * s, BS * s + 384), B("zc%d" % s), B("yp%d" % s, 0, 24))
        take("v", B(nxt, BS * s + 384, BS * s + BS), B("zc%d" % s), B("yp%d" % s, 24, 48))

    def border_take(win):
        take("s", B("sb", 0, 384), B(win, 0, P), B("sndu", 0, 24))
        take("v", B("sb", 384, NB), B(win, 0, P), B("sndu", 24, 42))

    fill(B("BO"), 1.0)
    fill(B("gb"), 0.0)
    fill(B("L"), 0.0)
    fill(B("I"), 1.0)
    dma("sync", B("sndi"), HB(T.snd[:, :]))
    dma("scalar", B("pk", 0, BS), HB(T.cd[:, 0:BS]))
    dma("sync", B("xw", 0, BS), HB(T.x[:, 0:BS]))
    dma("sync", B("gb", parts=slice(0, 128, 16)), HB(T.sd[:, :]))
    dma("sync", B("xw", BS, P), HB(T.x[:, BS:P]))
    dma("sync", B("tlb"), HB(T.tl[:, :]))
    fill(B("E"), 1.0)
    gsel(B("BO"), [[-16, 8], [0, 16]], OP.is_ge, 0, 1)
    gsel(B("BO"), [[16, 8], [0, 16]], OP.is_ge, 15, -1)
    gsel(B("NU"), [[-1, 128]], OP.is_gt, 0, 1, B("BO"))
    giota(B("pi"), [[0, 8]], 0, 1)
    giota(B("N256"), [[16, 48]], 256, 0)
    giota(B("dum"), [[0, 8], [4096, 32]], 4 * W * 256, 0)
    gsel(B("I"), [[-1, 128]], OP.is_equal, 0, 1)
    er = B("pk", 2 * BS, 2 * BS + NB)
    giota(er, [[1, NB]], 0, 0)
    gsel(B("E"), [[-1, 128], [0, 16]], OP.is_equal, 0, 1)
    for lo in range(0, P, 2048):
        hi = min(P, lo + 2048)
        act(B("inv", lo, hi), B("L", 0, hi - lo), AF.Copy, scale=0.0, bias=float(NB))
    for a in range(16):
        act(B("L", 128 * a + a, 128 * a + 128, 16), B("BO", a, 128, 16), AF.Copy)
    act(B("L32"), B("L"), AF.Copy)
    fill(B("z48"), 0.0)
    ts(B("NU"), B("NU"), -1.0, OP.mult)
    ts(B("pj"), B("pi"), 15, OP.bitwise_and)
    copy(B("pf15"), B("pj"))
    ts(B("pf15k"), B("pf15"), 256.0, OP.mult)
    ts(B("N256"), B("N256"), B("pf15", 0, 1), OP.add)
    ts(B("N769"), B("N256"), 513.0, OP.add)
    ts(B("dum"), B("dum"), B("pf15k", 0, 1), OP.add)
    copy(B("pkw", 1, 257), B("dum"))
    copy(B("sndu", 0, 42), B("sndi"))
    copy(IND(B("inv"), B("sndu", 0, 42)), er)
    pack(0)
    pe(chain(B("pf", 0, 48), [(Lm(a), B("gb", a, BS, 16)) for a in range(16)]))
    members(0)
    take("s", B("sb"), B("xw", 0, P), B("sndu", 0, 42))
    rx = send("x", "sb", "xw", P)
    dma("sync", B("yA", 0, P), HB(T.y0[:, :]), after=[rx])
    dma("sync", B("pk", BS, 2 * BS), HB(T.cd[:, BS:2 * BS]))
    for s in (2, 1, 0):
        dma("sync", B("zc%d" % s, 256, 1024), HB(T.y0[:, s * BS:s * BS + BS]))
    dma("sync", B("yB", 0, P), HB(T.y0[:, :]))
    dma("sync", B("pk", 2 * BS, 3 * BS), HB(T.cd[:, 2 * BS:3 * BS]))
    members2(0)
    numbers(0)
    fill(B("xw", W, WX), 0.0)
    zero("wA", 0, ZV, ZS, 20096 - ZV - ZS)
    for n, v in (("sm", 191.0), ("sx", 200.0)):
        fill(B(n), v)
    for s in range(3):
        fill(B("fr%d" % s, 672, 688), 0.0)
    fill(B("yA", W, WX), 0.0)
    fill(B("yB", W, WX), 0.0)
    ts(B("N257"), B("N256"), 1.0, OP.add)
    tabi = chain(B("pf", 0, 96), [(Lm(a, "L32"), B("inv", BS + a, 3 * BS, 16)) for a in range(16)])
    run(chunks("o", 0, "wA", range(NC), EG_OUT), {t: (lambda t=t: pe(tabi[4 * t - 16:4 * t - 12])) for t in range(4, 8)})
    gsel(B("sm"), [[0, 32], [1, 16]], OP.is_equal, 0, 0)
    gsel(B("sx"), [[0, 32], [1, 16]], OP.not_equal, 0, 0)
    zero("wB", 0, 0, 0, ZB)
    ts(B("invT"), B("pf", 0, 96), 0.0625, OP.mult)
    border_flags(0, "wA")
    pe(chain(B("pf", 0, 48), brood_table(1, "wA"), last=False))
    border_take("yA")
    send("y0", "sb", "yA", P)
    pack(1)
    places(0)
    zero("wB", ZB, 3500, 4096, 20096 - 3500 - 4096 - ZB)
    dma("sync", B("tq0"), B("wA", 0, 4 * P, parts=slice(0, 128, 16)))
    giota(B("cwin", 0, 256), [[0, 256]], 1, 0)
    giota(B("cwin", 256, 1024), [[0, 768]], 0, 0)
    zero("row", 0, 0, 0, P)
    zero("sdq", 0, 0, 0, 272)
    flags_in(0)
    members(1)
    tab2 = chain(B("pf", 0, 48), brood_table(2, "wA"))
    at = {t: (lambda t=t: pe(tab2[16 * t - 48:16 * t - 32])) for t in range(3, 7)}

    def mid1():
        members2(1)
        numbers(1)
    at[-1] = mid1
    run(chunks("o", 1, "wB", range(NC), EG_OUT), at)
    border_flags(1, "wB")
    copy(B("F2a"), B("pf", 0, 48))
    pe(chain(B("pf", 0, 48), brood_table(2, "wB") + [(B("I"), B("F2a"))], last=False))
    pack(2)
    places(1)
    zero("wA", 0, 4500, 2048, 20096 - 2048 - 4500)
    for s in (0, 1):
        take("s", B("row", s * BS, s * BS + BS), B("cwin"), B("yp%d" % s))
    dma("sync", B("tq1"), B("wB", 0, 4 * P, parts=slice(0, 128, 16)))
    for q in range(3):
        n = 272 if q < 2 else 224
        dma("sync", B("sdq", 0, n, parts=slice(q, 128, 16)), HB(T.sd[:, 272 * q:272 * q + n]))
    flags_in(1)
    members(2)

    def mid2():
        numbers(2)
        places(2)

    def after2():
        stand(2, "yB")
        border_take("yB")
        send("y1", "sb", "yB", P)
        dma("sync", B("yA", 2 * BS, 3 * BS), B("yB", 2 * BS, 3 * BS))
        dma("sync", HB(T.yv[:, 2 * BS:3 * BS]), B("yB", 2 * BS, 3 * BS))
    run(chunks("b", 2, "yA", range(NC), EG_BACK2) + chunks("o", 2, "wA", range(SPLIT), EG_OUT2), {-1: lambda: members2(2), 3: mid2}, after2)
    take("s", B("row", 2 * BS, 3 * BS), B("cwin"), B("yp2"))
    dma("sync", B("mq"), B("row", parts=slice(0, 128, 16)))
    zero("row", 0, 0, 0, 3 * BS)

    def after1():
        stand(1, "yA")
        border_take("yA")
        send("y2", "sb", "yA", P)
        dma("sync", HB(T.yv[:, BS:2 * BS]), B("yA", BS, 2 * BS))
    run(chunks("b", 1, "yB", range(NC), EG_BACK) + chunks("o", 2, "wA", range(SPLIT, NC), EG_OUT2), {}, after1)
    acc = B("pf", 0, 272)

    def flags_out():
        border_flags(2, "wA")
        dma("sync", B("tq2"), B("wA", 0, 4 * P, parts=slice(0, 128, 16)))

    def flags_own():
        pe(chain(acc, [(B("I"), B("tq%d" % s, k, 1088, 4)) for s in range(3) for k in range(4)] + [(B("I"), B("sdq"))], last=False))

    def flags_all():
        copy(IND(B("row"), B("sndu", 0, 42)), B("fr2", 0, NB))
        dma("sync", B("rbq"), B("row", parts=slice(0, 128, 16)))

    def flags_end():
        pe(chain(acc, [(B("I"), B("rbq"))], first=False))
        ts(B("yft"), acc, 0.5, OP.is_gt)
        tt(B("yfo"), B("yft"), B("mq"), OP.add)
        dma("sync", HB(T.yf[:, :]), B("yfo"))
    run(chunks("b", 0, "yA", range(NC), EG_BACK), {1: flags_out, 5: flags_own, 6: flags_all, 8: flags_end})
    stand(0, "yB")
    dma("scalar", HB(T.yv[:, 0:384]), B("yB", 0, 384))
    dma("sync", HB(T.yv[:, 384:BS]), B("yB", 384, BS))
    totals.update(count)
    for s in sorted(totals):
        if known["g"].get(s, 0) < totals[s]:
            g.wait_ge(T.sem[s], totals[s])
